import numpy as np
import ml_dtypes


def mxq(x, axis, fmt="e4m3"):
    dtype, down = {"e4m3": (ml_dtypes.float8_e4m3fn, 7), "e5m2": (ml_dtypes.float8_e5m2, 14)}[fmt]
    v = np.moveaxis(np.asarray(x, np.float32).astype(ml_dtypes.bfloat16).astype(np.float64), axis, -1)
    blocks = v.reshape(v.shape[:-1] + (-1, 32))
    amax = np.abs(blocks).max(-1, keepdims=True)
    byte = np.maximum(np.where(amax > 0, np.frexp(amax)[1] - 1 + 127, 0) - down, 1)
    scale = np.exp2(byte - 127.0)
    codes = (blocks / scale).astype(np.float32).astype(dtype).astype(np.float64)
    return np.moveaxis((codes * scale).reshape(v.shape), -1, axis)


WIDE = False


def mx_kscale(k):
    if not WIDE:
        return np.ones(k)
    levels = np.array([10, -10, 5, -5, 0])
    if k % 512:
        return np.exp2(np.random.permutation(np.resize(levels, k // 32))).repeat(32)
    a = np.empty((k // 512, 16))
    for p in range(k // 512):
        a[p, :8] = np.random.permutation(np.resize(levels, 8))
        for g in range(8):
            far = levels[np.abs(levels - a[p, g]) >= 10]
            a[p, g + 8] = far[np.random.randint(len(far))]
    return np.exp2(a.ravel()).repeat(32)


def f64(x):
    return np.asarray(x).astype(np.float64)


def striped(idx):
    return np.tile(np.asarray(idx).reshape(-1, 16).T, (8, 1)).astype(np.uint16)


def unstriped(offs):
    return offs[:16].T.reshape(-1).astype(np.int64)


B, N, T, D, DV, NQ = 1, 512, 1024, 1024, 256, 128


def setup_inputs():
    n = np.random.standard_normal
    idx = np.random.permutation(T)[:B * N]
    s = mx_kscale(D)[:, None]
    u = np.ones(T)
    u[idx] = mx_kscale(B * N)
    r = np.random.uniform(0.5, 2.0, T)
    k = n((D, T)) / s
    v = n((DV, T)) / (u * r)
    return {
        "qT": (n((B, D, NQ)) * s * (0.60 / np.sqrt(D))).astype(np.float32),
        "kT": k.astype(np.float32),
        "vT": v.astype(np.float32),
        "vs": np.tile(u * r, (128, 1)).astype(np.float32),
        "kb": np.tile(n(T), (128, 1)).astype(np.float32),
        "offs": striped(idx),
    }


def reference(qT, kT, vT, vs, kb, offs):
    idx = unstriped(offs)
    k = f64(kT)
    v = f64(vT)
    pick = lambda x: x[:, idx].reshape(x.shape[0], B, N).transpose(1, 0, 2)
    q = f64(qT)
    score = mxq(q, 1, "e4m3").transpose(0, 2, 1) @ mxq(pick(k), 1, "e4m3")
    score = score + pick(f64(kb))[:, :1, :]
    m = score.max(-1, keepdims=True)
    p = np.exp(score - m)
    total = p.sum(-1, keepdims=True)
    w = p * pick(f64(vs))[:, :1, :]
    y = mxq(w, 2, "e4m3") @ mxq(pick(v).transpose(0, 2, 1), 1, "e4m3")
    y = y / total
    return y

@@ -1,0 +1,192 @@
+from contextlib import ExitStack
+
+import concourse.mybir as mybir
+from concourse.masks import make_identity
+
+F32 = mybir.dt.float32
+BF16 = mybir.dt.bfloat16
+U32 = mybir.dt.uint32
+U16 = mybir.dt.uint16
+U8 = mybir.dt.uint8
+FP8X4 = mybir.dt.float8_e4m3fn_x4
+ACT = mybir.ActivationFunctionType
+ALU = mybir.AluOpType
+AX = mybir.AxisListType
+
+D, T, N, DV, NQ = 1024, 1024, 512, 256, 128
+P = 128
+PASSES = D // 512
+HALF = N // 2
+FLOPS = 2 * NQ * N * D + 2 * NQ * N * DV
+SHARES = {
+    (0, 0): [(0, 512, [("S", 256), ("V", 256)]), (512, 1024, [("S", 256), ("V", 256)])],
+    (0, 1): [(0, 1024, [("S", 608), ("G", 416)])],
+    (1, 0): [(0, 1024, [("S", 608), ("G", 416)])],
+    (1, 1): [(0, 512, [("S", 272), ("G", 240)]), (512, 1024, [("S", 160), ("G", 160), ("V", 192)])],
+}
+V_SHARES = [("S", 512), ("G", 512)]
+
+
+def tile_attend_x_wide_bias_topk_kernel(tc, qT, kT, vT, vs, kb, offs, out):
+    nc = tc.nc
+    with ExitStack() as ctx:
+        keep = ctx.enter_context(tc.tile_pool(name="keep", bufs=1))
+        psum = ctx.enter_context(tc.psum_pool(name="psum", bufs=1))
+
+        def cast(engine, dst, src):
+            if engine == "S":
+                nc.scalar.activation(dst, src, ACT.Copy)
+            elif engine == "V":
+                nc.vector.tensor_copy(dst, src)
+            else:
+                nc.gpsimd.tensor_copy(dst, src)
+
+        def cast_shares(shares, dst, src):
+            at = 0
+            for engine, width in shares:
+                cast(engine, dst[:, at : at + width], src[:, at : at + width])
+                at += width
+
+        offsets = keep.tile([P, N // 16], U16, name="offsets")
+        nc.sync.dma_start(offsets[:], offs)
+        warm = keep.tile([P, 1], F32, name="warm")
+        nc.vector.memset(warm[:], 0.0)
+        nc.scalar.activation(warm[:], warm[:], ACT.Exp)
+        kb_win = keep.tile([P, T], F32, name="kb_win")
+        nc.sync.dma_start(out=kb_win[:32, :], in_=kb[:32, :])
+        nc.vector.memset(kb_win[32:64, :], 0.0)
+        nc.vector.memset(kb_win[64:, :], 0.0)
+        vs_win = keep.tile([P, T], F32, name="vs_win")
+        nc.sync.dma_start(out=vs_win[:32, :], in_=vs[:32, :])
+        nc.gpsimd.memset(vs_win[32:64, :], 0.0)
+        nc.gpsimd.memset(vs_win[64:, :], 0.0)
+        q_raw = keep.tile([P, PASSES, 4, NQ], F32, name="q_raw")
+        nc.sync.dma_start(out=q_raw[:], in_=qT.rearrange("b (g p t) n -> p (b g) t n", g=PASSES, t=4))
+        k_rows = kT.rearrange("(g p t) n -> g p t n", g=PASSES, t=4)
+        k_raw = {}
+        for (g, u), pieces in SHARES.items():
+            for a, b, shares in pieces:
+                raw = keep.tile([P, 2, b - a], F32, name=f"k_raw_{g}_{u}_{a}")
+                nc.sync.dma_start(out=raw[:], in_=k_rows[g][:, 2 * u : 2 * u + 2, a:b])
+                k_raw[(g, u, a)] = raw
+        v_raw = keep.tile([P, 2, T], F32, name="v_raw", tag="v_raw")
+        nc.sync.dma_start(out=v_raw[:], in_=vT.rearrange("(h p) n -> p h n", h=2))
+
+        ident = keep.tile([P, P], F32, name="ident")
+        make_identity(nc, ident[:])
+        ident_bf = keep.tile([P, P], BF16, name="ident_bf")
+        make_identity(nc, ident_bf[:])
+
+        def spread(window, name):
+            picked = keep.tile([P, N], F32, name=f"{name}_picked")
+            nc.vector.tensor_copy(picked[:], window[:].indirect(offsets[:]))
+            turned = psum.tile([P, 4, P], F32, name=f"{name}_turned", tag=f"{name}_turned")
+            for c in range(4):
+                nc.tensor.transpose(turned[:, c, :], picked[:, c * P : (c + 1) * P], ident[:])
+            col = keep.tile([P, 4], F32, name=f"{name}_col")
+            nc.vector.tensor_copy(col[:], turned[:, :, 0])
+            rows = psum.tile([P, 4, P], F32, name=f"{name}_rows")
+            for c in range(4):
+                nc.tensor.transpose(rows[:, c, :], col[:, c : c + 1].to_broadcast([P, P]), ident[:])
+            return rows[:].rearrange("p c n -> p (c n)")
+
+        kb_rows = spread(kb_win, "kb")
+        vs_g = spread(vs_win, "vs")
+
+        q_bf = keep.tile([P, PASSES, NQ, 4], BF16, name="q_bf", align_bytes=64)
+        for g in range(PASSES):
+            cast("G", q_bf[:, g], q_raw[:, g].rearrange("p t n -> p n t"))
+        q_codes = keep.tile([P, PASSES * NQ], U32, name="q_codes", align_bytes=64)
+        q_scales = keep.tile([P, PASSES * NQ], U8, name="q_scales", align_bytes=64)
+        nc.vector.quantize_mx(out=q_codes[:].bitcast(FP8X4), scales=q_scales[:], in_=q_bf[:].rearrange("p g n t -> p (g n t)"))
+
+        kb_g = keep.tile([P, N], F32, name="kb_g")
+        s_bank = [psum.tile([P, 512], F32, name=f"s_bank{h}", tag=f"{x}_turned") for h, x in enumerate(["kb", "vs"])]
+        for g in range(PASSES):
+            k_g = keep.tile([P, N * 4], BF16, name=f"k_g{g}", align_bytes=64)
+            k_words = k_g[:].bitcast(U32).rearrange("p (n u) -> p n u", u=2)
+            for u in range(2):
+                pool_bf = keep.tile([P, T], U32, name=f"k_bf_{g}_{u}")
+                pairs = pool_bf[:].bitcast(BF16).rearrange("p (n j) -> p n j", j=2)
+                for a, b, shares in SHARES[(g, u)]:
+                    cast_shares(shares, pairs[:, a:b], k_raw[(g, u, a)][:].rearrange("p j n -> p n j"))
+                nc.vector.tensor_copy(k_words[:, :, u], pool_bf[:].indirect(offsets[:]))
+                if (g, u) == (0, 0):
+                    nc.scalar.activation(kb_g[:], kb_rows, ACT.Copy)
+            codes = keep.tile([P, N], U32, name=f"k_codes{g}", align_bytes=64)
+            scales = keep.tile([P, N], U8, name=f"k_scales{g}", align_bytes=64)
+            for h in range(2):
+                cols = slice(h * HALF, (h + 1) * HALF)
+                nc.vector.quantize_mx(
+                    out=codes[:, cols].bitcast(FP8X4),
+                    scales=scales[:, cols],
+                    in_=k_g[:, h * HALF * 4 : (h + 1) * HALF * 4],
+                )
+                nc.tensor.matmul_mx(
+                    out=s_bank[h][:, :HALF],
+                    lhsT=q_codes[:, g * NQ : (g + 1) * NQ].bitcast(FP8X4),
+                    lhsT_scale=q_scales[:, g * NQ : (g + 1) * NQ],
+                    rhs=codes[:, cols].bitcast(FP8X4),
+                    rhs_scale=scales[:, cols],
+                    start=(g == 0),
+                    stop=(g == PASSES - 1),
+                )
+
+        v_bf = keep.tile([P, T], U32, name="v_bf")
+        cast_shares(V_SHARES, v_bf[:].bitcast(BF16).rearrange("p (n h) -> p n h", h=2), v_raw[:].rearrange("p h n -> p n h"))
+
+        s = keep.tile([P, N], F32, name="s")
+        for h in range(2):
+            cols = slice(h * HALF, (h + 1) * HALF)
+            nc.vector.tensor_tensor(s[:, cols], s_bank[h][:, :HALF], kb_g[:, cols], ALU.add)
+        neg_m = keep.tile([P, 1], F32, name="neg_m")
+        nc.vector.tensor_reduce(neg_m[:], s[:], AX.X, ALU.max, negate=True)
+        p = keep.tile([P, N], F32, name="p", tag="v_raw")
+        w = keep.tile([P, N], BF16, name="w", align_bytes=64)
+        parts = [keep.tile([P, 1], F32, name=f"l_part{h}") for h in range(2)]
+        for h in range(2):
+            cols = slice(h * HALF, (h + 1) * HALF)
+            nc.scalar.activation(p[:, cols], s[:, cols], ACT.Exp, bias=neg_m[:], accum_out=parts[h][:])
+        v_g = keep.tile([P, N], U32, name="v_g", align_bytes=64)
+        nc.vector.tensor_copy(v_g[:], v_bf[:].indirect(offsets[:]))
+        for h in range(2):
+            cols = slice(h * HALF, (h + 1) * HALF)
+            nc.vector.tensor_tensor(w[:, cols], p[:, cols], vs_g[:, cols], ALU.mult)
+        w_bank = psum.tile([P, 4, P], BF16, name="w_bank", padded_shape=[P, 8, P])
+        w_slots = w[:].rearrange("p (s t) -> p t s", t=4)
+        for t in range(4):
+            nc.tensor.transpose(w_bank[:, t, :], w_slots[:, t, :], ident_bf[:])
+        w_t = keep.tile([P, NQ, 4], BF16, name="w_t", align_bytes=64)
+        nc.vector.tensor_copy(w_t[:], w_bank[:].rearrange("p t q -> p q t"))
+        w_codes = keep.tile([P, NQ], U32, name="w_codes", align_bytes=64)
+        w_scales = keep.tile([P, NQ], U8, name="w_scales", align_bytes=64)
+        nc.vector.quantize_mx(out=w_codes[:].bitcast(FP8X4), scales=w_scales[:], in_=w_t[:].rearrange("p q t -> p (q t)"))
+        total = keep.tile([P, 1], F32, name="total")
+        nc.vector.tensor_tensor(total[:], parts[0][:], parts[1][:], ALU.add)
+        inv = keep.tile([P, 1], F32, name="inv")
+        nc.vector.reciprocal(inv[:], total[:])
+
+        v_bank = psum.tile([P, 4, DV], BF16, name="v_bank")
+        v_slots = v_g[:].bitcast(BF16).rearrange("p (s t h) -> p t h s", t=4, h=2)
+        for t in range(4):
+            for h in range(2):
+                nc.tensor.transpose(v_bank[:, t, h * P : (h + 1) * P], v_slots[:, t, h, :], ident_bf[:])
+        v_t = keep.tile([P, DV, 4], BF16, name="v_t", align_bytes=64)
+        nc.scalar.copy(v_t[:], v_bank[:].rearrange("p t e -> p e t"))
+        v_codes = keep.tile([P, DV], U32, name="v_codes", align_bytes=64)
+        v_scales = keep.tile([P, DV], U8, name="v_scales", align_bytes=64)
+        nc.vector.quantize_mx(out=v_codes[:].bitcast(FP8X4), scales=v_scales[:], in_=v_t[:].rearrange("p e t -> p (e t)"))
+
+        y_bank = psum.tile([P, DV], F32, name="y_bank", padded_shape=[P, 512])
+        nc.tensor.matmul_mx(
+            out=y_bank[:],
+            lhsT=w_codes[:].bitcast(FP8X4),
+            lhsT_scale=w_scales[:],
+            rhs=v_codes[:].bitcast(FP8X4),
+            rhs_scale=v_scales[:],
+            start=True,
+            stop=True,
+        )
+        y = keep.tile([P, DV], F32, name="y")
+        nc.vector.tensor_scalar(y[:], y_bank[:], inv[:], None, ALU.mult)
+        nc.sync.dma_start(out=out.rearrange("b q e -> (b q) e"), in_=y[:])

@@ -19,12 +19,12 @@ PASSES = D // 512
 HALF = N // 2
 FLOPS = 2 * NQ * N * D + 2 * NQ * N * DV
 SHARES = {
-    (0, 0): [(0, 512, [("S", 256), ("V", 256)]), (512, 1024, [("S", 256), ("V", 256)])],
-    (0, 1): [(0, 1024, [("S", 608), ("G", 416)])],
-    (1, 0): [(0, 1024, [("S", 608), ("G", 416)])],
-    (1, 1): [(0, 512, [("S", 272), ("G", 240)]), (512, 1024, [("S", 160), ("G", 160), ("V", 192)])],
+    (0, 0): [(0, 512, [("S", 512)]), (512, 1024, [("V", 512)])],
+    (0, 1): [(0, 512, [("S", 512)]), (512, 1024, [("S", 256), ("V", 256)])],
+    (1, 0): [(0, 512, [("S", 512)]), (512, 1024, [("S", 312), ("V", 200)])],
+    (1, 1): [(0, 512, [("S", 512)]), (512, 1024, [("S", 256), ("V", 256)])],
 }
-V_SHARES = [("S", 512), ("G", 512)]
+V_SHARES = [(0, 512, [("S", 512)]), (512, 1024, [("S", 512)])]
 
 
 def tile_attend_x_wide_bias_topk_kernel(tc, qT, kT, vT, vs, kb, offs, out):
@@ -39,7 +39,7 @@ def tile_attend_x_wide_bias_topk_kernel(tc, qT, kT, vT, vs, kb, offs, out):
             elif engine == "V":
                 nc.vector.tensor_copy(dst, src)
             else:
-                nc.gpsimd.tensor_copy(dst, src)
+                nc.gpsimd.tensor_scalar(dst, src, 1.0, 0.0, ALU.mult, ALU.add)
 
         def cast_shares(shares, dst, src):
             at = 0
@@ -61,7 +61,6 @@ def tile_attend_x_wide_bias_topk_kernel(tc, qT, kT, vT, vs, kb, offs, out):
         nc.gpsimd.memset(vs_win[32:64, :], 0.0)
         nc.gpsimd.memset(vs_win[64:, :], 0.0)
         q_raw = keep.tile([P, PASSES, 4, NQ], F32, name="q_raw")
-        nc.sync.dma_start(out=q_raw[:], in_=qT.rearrange("b (g p t) n -> p (b g) t n", g=PASSES, t=4))
         k_rows = kT.rearrange("(g p t) n -> g p t n", g=PASSES, t=4)
         k_raw = {}
         for (g, u), pieces in SHARES.items():
@@ -69,8 +68,12 @@ def tile_attend_x_wide_bias_topk_kernel(tc, qT, kT, vT, vs, kb, offs, out):
                 raw = keep.tile([P, 2, b - a], F32, name=f"k_raw_{g}_{u}_{a}")
                 nc.sync.dma_start(out=raw[:], in_=k_rows[g][:, 2 * u : 2 * u + 2, a:b])
                 k_raw[(g, u, a)] = raw
-        v_raw = keep.tile([P, 2, T], F32, name="v_raw", tag="v_raw")
-        nc.sync.dma_start(out=v_raw[:], in_=vT.rearrange("(h p) n -> p h n", h=2))
+        nc.sync.dma_start(out=q_raw[:], in_=qT.rearrange("b (g p t) n -> p (b g) t n", g=PASSES, t=4))
+        v_raw = []
+        for a, b, shares in V_SHARES:
+            raw = keep.tile([P, 2, b - a], F32, name=f"v_raw_{a}", tag=f"v_raw_{b}")
+            nc.sync.dma_start(out=raw[:], in_=vT.rearrange("(h p) n -> p h n", h=2)[:, :, a:b])
+            v_raw.append(raw)
 
         ident = keep.tile([P, P], F32, name="ident")
         make_identity(nc, ident[:])
@@ -84,7 +87,7 @@ def tile_attend_x_wide_bias_topk_kernel(tc, qT, kT, vT, vs, kb, offs, out):
             for c in range(4):
                 nc.tensor.transpose(turned[:, c, :], picked[:, c * P : (c + 1) * P], ident[:])
             col = keep.tile([P, 4], F32, name=f"{name}_col")
-            nc.vector.tensor_copy(col[:], turned[:, :, 0])
+            nc.scalar.activation(col[:], turned[:, :, 0], ACT.Copy)
             rows = psum.tile([P, 4, P], F32, name=f"{name}_rows")
             for c in range(4):
                 nc.tensor.transpose(rows[:, c, :], col[:, c : c + 1].to_broadcast([P, P]), ident[:])
@@ -93,47 +96,56 @@ def tile_attend_x_wide_bias_topk_kernel(tc, qT, kT, vT, vs, kb, offs, out):
         kb_rows = spread(kb_win, "kb")
         vs_g = spread(vs_win, "vs")
 
+        kb_g = keep.tile([P, N], F32, name="kb_g")
+        k_g = [keep.tile([P, N * 4], BF16, name=f"k_g{g}", align_bytes=64) for g in range(PASSES)]
+        k_codes = [keep.tile([P, N], U32, name=f"k_codes{g}", align_bytes=64) for g in range(PASSES)]
+        k_scales = [keep.tile([P, N], U8, name=f"k_scales{g}", align_bytes=64) for g in range(PASSES)]
+
+        def quantize_keys(g, cols):
+            nc.vector.quantize_mx(
+                out=k_codes[g][:, cols].bitcast(FP8X4),
+                scales=k_scales[g][:, cols],
+                in_=k_g[g][:, cols.start * 4 : cols.stop * 4],
+            )
+
+        for (g, u), pieces in SHARES.items():
+            pool_bf = keep.tile([P, T], U32, name=f"k_bf_{g}_{u}")
+            pairs = pool_bf[:].bitcast(BF16).rearrange("p (n j) -> p n j", j=2)
+            for a, b, shares in pieces:
+                cast_shares(shares, pairs[:, a:b], k_raw[(g, u, a)][:].rearrange("p j n -> p n j"))
+            words = k_g[g][:].bitcast(U32).rearrange("p (n u) -> p n u", u=2)
+            nc.vector.tensor_copy(words[:, :, u], pool_bf[:].indirect(offsets[:]))
+            if (g, u) == (0, 0):
+                nc.vector.tensor_copy(kb_g[:], kb_rows)
+            if (g, u) == (0, 1):
+                quantize_keys(0, slice(0, N))
+
         q_bf = keep.tile([P, PASSES, NQ, 4], BF16, name="q_bf", align_bytes=64)
         for g in range(PASSES):
-            cast("G", q_bf[:, g], q_raw[:, g].rearrange("p t n -> p n t"))
+            cast("SG"[g], q_bf[:, g], q_raw[:, g].rearrange("p t n -> p n t"))
         q_codes = keep.tile([P, PASSES * NQ], U32, name="q_codes", align_bytes=64)
         q_scales = keep.tile([P, PASSES * NQ], U8, name="q_scales", align_bytes=64)
         nc.vector.quantize_mx(out=q_codes[:].bitcast(FP8X4), scales=q_scales[:], in_=q_bf[:].rearrange("p g n t -> p (g n t)"))
 
-        kb_g = keep.tile([P, N], F32, name="kb_g")
         s_bank = [psum.tile([P, 512], F32, name=f"s_bank{h}", tag=f"{x}_turned") for h, x in enumerate(["kb", "vs"])]
-        for g in range(PASSES):
-            k_g = keep.tile([P, N * 4], BF16, name=f"k_g{g}", align_bytes=64)
-            k_words = k_g[:].bitcast(U32).rearrange("p (n u) -> p n u", u=2)
-            for u in range(2):
-                pool_bf = keep.tile([P, T], U32, name=f"k_bf_{g}_{u}")
-                pairs = pool_bf[:].bitcast(BF16).rearrange("p (n j) -> p n j", j=2)
-                for a, b, shares in SHARES[(g, u)]:
-                    cast_shares(shares, pairs[:, a:b], k_raw[(g, u, a)][:].rearrange("p j n -> p n j"))
-                nc.vector.tensor_copy(k_words[:, :, u], pool_bf[:].indirect(offsets[:]))
-                if (g, u) == (0, 0):
-                    nc.scalar.activation(kb_g[:], kb_rows, ACT.Copy)
-            codes = keep.tile([P, N], U32, name=f"k_codes{g}", align_bytes=64)
-            scales = keep.tile([P, N], U8, name=f"k_scales{g}", align_bytes=64)
-            for h in range(2):
-                cols = slice(h * HALF, (h + 1) * HALF)
-                nc.vector.quantize_mx(
-                    out=codes[:, cols].bitcast(FP8X4),
-                    scales=scales[:, cols],
-                    in_=k_g[:, h * HALF * 4 : (h + 1) * HALF * 4],
-                )
+        for h in range(2):
+            cols = slice(h * HALF, (h + 1) * HALF)
+            quantize_keys(1, cols)
+            for g in range(PASSES):
                 nc.tensor.matmul_mx(
                     out=s_bank[h][:, :HALF],
                     lhsT=q_codes[:, g * NQ : (g + 1) * NQ].bitcast(FP8X4),
                     lhsT_scale=q_scales[:, g * NQ : (g + 1) * NQ],
-                    rhs=codes[:, cols].bitcast(FP8X4),
-                    rhs_scale=scales[:, cols],
+                    rhs=k_codes[g][:, cols].bitcast(FP8X4),
+                    rhs_scale=k_scales[g][:, cols],
                     start=(g == 0),
                     stop=(g == PASSES - 1),
                 )
 
         v_bf = keep.tile([P, T], U32, name="v_bf")
-        cast_shares(V_SHARES, v_bf[:].bitcast(BF16).rearrange("p (n h) -> p n h", h=2), v_raw[:].rearrange("p h n -> p n h"))
+        v_pairs = v_bf[:].bitcast(BF16).rearrange("p (n h) -> p n h", h=2)
+        for (a, b, shares), raw in zip(V_SHARES, v_raw):
+            cast_shares(shares, v_pairs[:, a:b], raw[:].rearrange("p h n -> p n h"))
 
         s = keep.tile([P, N], F32, name="s")
         for h in range(2):
@@ -141,7 +153,7 @@ def tile_attend_x_wide_bias_topk_kernel(tc, qT, kT, vT, vs, kb, offs, out):
             nc.vector.tensor_tensor(s[:, cols], s_bank[h][:, :HALF], kb_g[:, cols], ALU.add)
         neg_m = keep.tile([P, 1], F32, name="neg_m")
         nc.vector.tensor_reduce(neg_m[:], s[:], AX.X, ALU.max, negate=True)
-        p = keep.tile([P, N], F32, name="p", tag="v_raw")
+        p = keep.tile([P, N], F32, name="p", tag="v_raw_1024")
         w = keep.tile([P, N], BF16, name="w", align_bytes=64)
         parts = [keep.tile([P, 1], F32, name=f"l_part{h}") for h in range(2)]
         for h in range(2):

@@ -20,11 +20,11 @@ HALF = N // 2
 FLOPS = 2 * NQ * N * D + 2 * NQ * N * DV
 SHARES = {
     (0, 0): [(0, 512, [("S", 512)]), (512, 1024, [("V", 512)])],
-    (0, 1): [(0, 512, [("S", 512)]), (512, 1024, [("S", 256), ("V", 256)])],
-    (1, 0): [(0, 512, [("S", 512)]), (512, 1024, [("S", 312), ("V", 200)])],
+    (0, 1): [(0, 1024, [("S", 768), ("V", 256)])],
+    (1, 0): [(0, 1024, [("S", 768), ("V", 256)])],
     (1, 1): [(0, 512, [("S", 512)]), (512, 1024, [("S", 256), ("V", 256)])],
 }
-V_SHARES = [(0, 512, [("S", 512)]), (512, 1024, [("S", 512)])]
+V_SHARES = [(0, 1024, [("S", 1024)])]
 
 
 def tile_attend_x_wide_bias_topk_kernel(tc, qT, kT, vT, vs, kb, offs, out):
@@ -47,6 +47,11 @@ def tile_attend_x_wide_bias_topk_kernel(tc, qT, kT, vT, vs, kb, offs, out):
                 cast(engine, dst[:, at : at + width], src[:, at : at + width])
                 at += width
 
+        ident = keep.tile([P, P], F32, name="ident")
+        make_identity(nc, ident[:])
+        ident_bf = keep.tile([P, P], BF16, name="ident_bf")
+        make_identity(nc, ident_bf[:])
+
         offsets = keep.tile([P, N // 16], U16, name="offsets")
         nc.sync.dma_start(offsets[:], offs)
         warm = keep.tile([P, 1], F32, name="warm")
@@ -58,8 +63,8 @@ def tile_attend_x_wide_bias_topk_kernel(tc, qT, kT, vT, vs, kb, offs, out):
         nc.vector.memset(kb_win[64:, :], 0.0)
         vs_win = keep.tile([P, T], F32, name="vs_win")
         nc.sync.dma_start(out=vs_win[:32, :], in_=vs[:32, :])
-        nc.gpsimd.memset(vs_win[32:64, :], 0.0)
-        nc.gpsimd.memset(vs_win[64:, :], 0.0)
+        nc.vector.memset(vs_win[32:64, :], 0.0)
+        nc.vector.memset(vs_win[64:, :], 0.0)
         q_raw = keep.tile([P, PASSES, 4, NQ], F32, name="q_raw")
         k_rows = kT.rearrange("(g p t) n -> g p t n", g=PASSES, t=4)
         k_raw = {}
@@ -72,13 +77,8 @@ def tile_attend_x_wide_bias_topk_kernel(tc, qT, kT, vT, vs, kb, offs, out):
         v_raw = []
         for a, b, shares in V_SHARES:
             raw = keep.tile([P, 2, b - a], F32, name=f"v_raw_{a}", tag=f"v_raw_{b}")
-            nc.sync.dma_start(out=raw[:], in_=vT.rearrange("(h p) n -> p h n", h=2)[:, :, a:b])
+            nc.sync.dma_start(out=raw[:], in_=vT.rearrange("(p h) n -> p h n", h=2)[:, :, a:b])
             v_raw.append(raw)
-
-        ident = keep.tile([P, P], F32, name="ident")
-        make_identity(nc, ident[:])
-        ident_bf = keep.tile([P, P], BF16, name="ident_bf")
-        make_identity(nc, ident_bf[:])
 
         def spread(window, name):
             picked = keep.tile([P, N], F32, name=f"{name}_picked")
@@ -169,7 +169,7 @@ def tile_attend_x_wide_bias_topk_kernel(tc, qT, kT, vT, vs, kb, offs, out):
         for t in range(4):
             nc.tensor.transpose(w_bank[:, t, :], w_slots[:, t, :], ident_bf[:])
         w_t = keep.tile([P, NQ, 4], BF16, name="w_t", align_bytes=64)
-        nc.vector.tensor_copy(w_t[:], w_bank[:].rearrange("p t q -> p q t"))
+        nc.scalar.copy(w_t[:], w_bank[:].rearrange("p t q -> p q t"))
         w_codes = keep.tile([P, NQ], U32, name="w_codes", align_bytes=64)
         w_scales = keep.tile([P, NQ], U8, name="w_scales", align_bytes=64)
         nc.vector.quantize_mx(out=w_codes[:].bitcast(FP8X4), scales=w_scales[:], in_=w_t[:].rearrange("p q t -> p (q t)"))
@@ -200,5 +200,7 @@ def tile_attend_x_wide_bias_topk_kernel(tc, qT, kT, vT, vs, kb, offs, out):
             stop=True,
         )
         y = keep.tile([P, DV], F32, name="y")
-        nc.vector.tensor_scalar(y[:], y_bank[:], inv[:], None, ALU.mult)
+        nc.vector.tensor_scalar(
+            y[:].rearrange("q (p h) -> q p h", h=2), y_bank[:].rearrange("q (h p) -> q p h", h=2), inv[:], None, ALU.mult
+        )
         nc.sync.dma_start(out=out.rearrange("b q e -> (b q) e"), in_=y[:])

@@ -6,6 +6,7 @@ from concourse.masks import make_identity
 F32 = mybir.dt.float32
 BF16 = mybir.dt.bfloat16
 U32 = mybir.dt.uint32
+I32 = mybir.dt.int32
 U16 = mybir.dt.uint16
 U8 = mybir.dt.uint8
 FP8X4 = mybir.dt.float8_e4m3fn_x4
@@ -19,12 +20,12 @@ PASSES = D // 512
 HALF = N // 2
 FLOPS = 2 * NQ * N * D + 2 * NQ * N * DV
 SHARES = {
-    (0, 0): [(0, 512, [("S", 512)]), (512, 1024, [("V", 512)])],
-    (0, 1): [(0, 1024, [("S", 768), ("V", 256)])],
-    (1, 0): [(0, 1024, [("S", 768), ("V", 256)])],
-    (1, 1): [(0, 512, [("S", 512)]), (512, 1024, [("S", 256), ("V", 256)])],
+    (0, 0): [(0, 1024, [("S", 448), ("V", 576)])],
+    (0, 1): [(0, 1024, [("S", 800), ("V", 224)])],
+    (1, 0): [(0, 1024, [("S", 800), ("V", 224)])],
+    (1, 1): [(0, 1024, [("S", 672), ("V", 352)])],
 }
-V_SHARES = [(0, 1024, [("S", 1024)])]
+V_SHARES = [(0, 512, [("S", 512)]), (512, 1024, [("S", 512)])]
 
 
 def tile_attend_x_wide_bias_topk_kernel(tc, qT, kT, vT, vs, kb, offs, out):
@@ -49,8 +50,6 @@ def tile_attend_x_wide_bias_topk_kernel(tc, qT, kT, vT, vs, kb, offs, out):
 
         ident = keep.tile([P, P], F32, name="ident")
         make_identity(nc, ident[:])
-        ident_bf = keep.tile([P, P], BF16, name="ident_bf")
-        make_identity(nc, ident_bf[:])
 
         offsets = keep.tile([P, N // 16], U16, name="offsets")
         nc.sync.dma_start(offsets[:], offs)
@@ -63,8 +62,8 @@ def tile_attend_x_wide_bias_topk_kernel(tc, qT, kT, vT, vs, kb, offs, out):
         nc.vector.memset(kb_win[64:, :], 0.0)
         vs_win = keep.tile([P, T], F32, name="vs_win")
         nc.sync.dma_start(out=vs_win[:32, :], in_=vs[:32, :])
-        nc.vector.memset(vs_win[32:64, :], 0.0)
-        nc.vector.memset(vs_win[64:, :], 0.0)
+        nc.gpsimd.memset(vs_win[32:64, :], 0.0)
+        nc.gpsimd.memset(vs_win[64:, :], 0.0)
         q_raw = keep.tile([P, PASSES, 4, NQ], F32, name="q_raw")
         k_rows = kT.rearrange("(g p t) n -> g p t n", g=PASSES, t=4)
         k_raw = {}
@@ -79,6 +78,9 @@ def tile_attend_x_wide_bias_topk_kernel(tc, qT, kT, vT, vs, kb, offs, out):
             raw = keep.tile([P, 2, b - a], F32, name=f"v_raw_{a}", tag=f"v_raw_{b}")
             nc.sync.dma_start(out=raw[:], in_=vT.rearrange("(p h) n -> p h n", h=2)[:, :, a:b])
             v_raw.append(raw)
+
+        ident_bf = keep.tile([P, P], BF16, name="ident_bf")
+        make_identity(nc, ident_bf[:])
 
         def spread(window, name):
             picked = keep.tile([P, N], F32, name=f"{name}_picked")
@@ -98,8 +100,14 @@ def tile_attend_x_wide_bias_topk_kernel(tc, qT, kT, vT, vs, kb, offs, out):
 
         kb_g = keep.tile([P, N], F32, name="kb_g")
         k_g = [keep.tile([P, N * 4], BF16, name=f"k_g{g}", align_bytes=64) for g in range(PASSES)]
+        k_words = [keep.tile([P, 2, N], U32, name=f"k_words{g}") for g in range(PASSES)]
         k_codes = [keep.tile([P, N], U32, name=f"k_codes{g}", align_bytes=64) for g in range(PASSES)]
         k_scales = [keep.tile([P, N], U8, name=f"k_scales{g}", align_bytes=64) for g in range(PASSES)]
+
+        def interleave_keys(g, cols):
+            dst = k_g[g][:].bitcast(I32).rearrange("p (n u) -> p n u", u=2)[:, cols, :]
+            src = k_words[g][:].rearrange("p u n -> p (u n)").bitcast(I32).rearrange("p (u n) -> p n u", u=2)[:, cols, :]
+            nc.vector.tensor_copy(dst, src)
 
         def quantize_keys(g, cols):
             nc.vector.quantize_mx(
@@ -113,11 +121,12 @@ def tile_attend_x_wide_bias_topk_kernel(tc, qT, kT, vT, vs, kb, offs, out):
             pairs = pool_bf[:].bitcast(BF16).rearrange("p (n j) -> p n j", j=2)
             for a, b, shares in pieces:
                 cast_shares(shares, pairs[:, a:b], k_raw[(g, u, a)][:].rearrange("p j n -> p n j"))
-            words = k_g[g][:].bitcast(U32).rearrange("p (n u) -> p n u", u=2)
-            nc.vector.tensor_copy(words[:, :, u], pool_bf[:].indirect(offsets[:]))
+            if (g, u) == (1, 0):
+                interleave_keys(0, slice(0, N))
+            nc.vector.tensor_copy(k_words[g][:, u, :], pool_bf[:].indirect(offsets[:]))
             if (g, u) == (0, 0):
-                nc.vector.tensor_copy(kb_g[:], kb_rows)
-            if (g, u) == (0, 1):
+                nc.scalar.activation(kb_g[:], kb_rows, ACT.Copy)
+            if (g, u) == (1, 0):
                 quantize_keys(0, slice(0, N))
 
         q_bf = keep.tile([P, PASSES, NQ, 4], BF16, name="q_bf", align_bytes=64)
@@ -128,8 +137,10 @@ def tile_attend_x_wide_bias_topk_kernel(tc, qT, kT, vT, vs, kb, offs, out):
         nc.vector.quantize_mx(out=q_codes[:].bitcast(FP8X4), scales=q_scales[:], in_=q_bf[:].rearrange("p g n t -> p (g n t)"))
 
         s_bank = [psum.tile([P, 512], F32, name=f"s_bank{h}", tag=f"{x}_turned") for h, x in enumerate(["kb", "vs"])]
-        for h in range(2):
-            cols = slice(h * HALF, (h + 1) * HALF)
+        halves = [slice(h * HALF, (h + 1) * HALF) for h in range(2)]
+        for cols in halves:
+            interleave_keys(1, cols)
+        for h, cols in enumerate(halves):
             quantize_keys(1, cols)
             for g in range(PASSES):
                 nc.tensor.matmul_mx(
@@ -147,6 +158,10 @@ def tile_attend_x_wide_bias_topk_kernel(tc, qT, kT, vT, vs, kb, offs, out):
         for (a, b, shares), raw in zip(V_SHARES, v_raw):
             cast_shares(shares, v_pairs[:, a:b], raw[:].rearrange("p h n -> p n h"))
 
+        v_g = keep.tile([P, N], U32, name="v_g", align_bytes=64)
+        v_slots = v_g[:].rearrange("p (t s) -> p s t", t=4)
+        nc.vector.tensor_copy(v_slots[:, : HALF // 4, :], v_bf[:].indirect(offsets[:, :16]))
+
         s = keep.tile([P, N], F32, name="s")
         for h in range(2):
             cols = slice(h * HALF, (h + 1) * HALF)
@@ -155,19 +170,18 @@ def tile_attend_x_wide_bias_topk_kernel(tc, qT, kT, vT, vs, kb, offs, out):
         nc.vector.tensor_reduce(neg_m[:], s[:], AX.X, ALU.max, negate=True)
         p = keep.tile([P, N], F32, name="p", tag="v_raw_1024")
         w = keep.tile([P, N], BF16, name="w", align_bytes=64)
+        w_slots = w[:].rearrange("p (t s) -> p s t", t=4)
         parts = [keep.tile([P, 1], F32, name=f"l_part{h}") for h in range(2)]
         for h in range(2):
             cols = slice(h * HALF, (h + 1) * HALF)
             nc.scalar.activation(p[:, cols], s[:, cols], ACT.Exp, bias=neg_m[:], accum_out=parts[h][:])
-        v_g = keep.tile([P, N], U32, name="v_g", align_bytes=64)
-        nc.vector.tensor_copy(v_g[:], v_bf[:].indirect(offsets[:]))
+        nc.vector.tensor_copy(v_slots[:, HALF // 4 :, :], v_bf[:].indirect(offsets[:, 16:32]))
         for h in range(2):
             cols = slice(h * HALF, (h + 1) * HALF)
-            nc.vector.tensor_tensor(w[:, cols], p[:, cols], vs_g[:, cols], ALU.mult)
+            nc.vector.tensor_tensor(w_slots[:, h * HALF // 4 : (h + 1) * HALF // 4, :], p[:, cols], vs_g[:, cols], ALU.mult)
         w_bank = psum.tile([P, 4, P], BF16, name="w_bank", padded_shape=[P, 8, P])
-        w_slots = w[:].rearrange("p (s t) -> p t s", t=4)
         for t in range(4):
-            nc.tensor.transpose(w_bank[:, t, :], w_slots[:, t, :], ident_bf[:])
+            nc.tensor.transpose(w_bank[:, t, :], w[:, t * P : (t + 1) * P], ident_bf[:])
         w_t = keep.tile([P, NQ, 4], BF16, name="w_t", align_bytes=64)
         nc.scalar.copy(w_t[:], w_bank[:].rearrange("p t q -> p q t"))
         w_codes = keep.tile([P, NQ], U32, name="w_codes", align_bytes=64)
@@ -178,13 +192,11 @@ def tile_attend_x_wide_bias_topk_kernel(tc, qT, kT, vT, vs, kb, offs, out):
         inv = keep.tile([P, 1], F32, name="inv")
         nc.vector.reciprocal(inv[:], total[:])
 
-        v_bank = psum.tile([P, 4, DV], BF16, name="v_bank")
-        v_slots = v_g[:].bitcast(BF16).rearrange("p (s t h) -> p t h s", t=4, h=2)
+        v_bank = psum.tile([P, 4 * P], F32, name="v_bank")
         for t in range(4):
-            for h in range(2):
-                nc.tensor.transpose(v_bank[:, t, h * P : (h + 1) * P], v_slots[:, t, h, :], ident_bf[:])
+            nc.tensor.transpose(v_bank[:, t * P : (t + 1) * P], v_g[:, t * P : (t + 1) * P].bitcast(F32), ident[:])
         v_t = keep.tile([P, DV, 4], BF16, name="v_t", align_bytes=64)
-        nc.scalar.copy(v_t[:], v_bank[:].rearrange("p t e -> p e t"))
+        nc.vector.tensor_copy(v_t[:], v_bank[:].bitcast(BF16).rearrange("p (t e) -> p e t", t=4))
         v_codes = keep.tile([P, DV], U32, name="v_codes", align_bytes=64)
         v_scales = keep.tile([P, DV], U8, name="v_scales", align_bytes=64)
         nc.vector.quantize_mx(out=v_codes[:].bitcast(FP8X4), scales=v_scales[:], in_=v_t[:].rearrange("p e t -> p (e t)"))
@@ -200,7 +212,5 @@ def tile_attend_x_wide_bias_topk_kernel(tc, qT, kT, vT, vs, kb, offs, out):
             stop=True,
         )
         y = keep.tile([P, DV], F32, name="y")
-        nc.vector.tensor_scalar(
-            y[:].rearrange("q (p h) -> q p h", h=2), y_bank[:].rearrange("q (h p) -> q p h", h=2), inv[:], None, ALU.mult
-        )
+        nc.vector.tensor_scalar(y[:], y_bank[:], inv[:], None, ALU.mult)
         nc.sync.dma_start(out=out.rearrange("b q e -> (b q) e"), in_=y[:])

from contextlib import ExitStack

import concourse.mybir as mybir
from concourse.masks import make_identity

F32 = mybir.dt.float32
BF16 = mybir.dt.bfloat16
U32 = mybir.dt.uint32
I32 = mybir.dt.int32
U16 = mybir.dt.uint16
U8 = mybir.dt.uint8
FP8X4 = mybir.dt.float8_e4m3fn_x4
ACT = mybir.ActivationFunctionType
ALU = mybir.AluOpType
AX = mybir.AxisListType

D, T, N, DV, NQ = 1024, 1024, 512, 256, 128
P = 128
PASSES = D // 512
HALF = N // 2
FLOPS = 2 * NQ * N * D + 2 * NQ * N * DV
SHARES = {
    (0, 0): [(0, 1024, [("S", 448), ("V", 576)])],
    (0, 1): [(0, 1024, [("S", 800), ("V", 224)])],
    (1, 0): [(0, 1024, [("S", 800), ("V", 224)])],
    (1, 1): [(0, 1024, [("S", 672), ("V", 352)])],
}
V_SHARES = [(0, 512, [("S", 512)]), (512, 1024, [("S", 512)])]


def tile_attend_x_wide_bias_topk_kernel(tc, qT, kT, vT, vs, kb, offs, out):
    nc = tc.nc
    with ExitStack() as ctx:
        keep = ctx.enter_context(tc.tile_pool(name="keep", bufs=1))
        psum = ctx.enter_context(tc.psum_pool(name="psum", bufs=1))

        def cast(engine, dst, src):
            if engine == "S":
                nc.scalar.activation(dst, src, ACT.Copy)
            elif engine == "V":
                nc.vector.tensor_copy(dst, src)
            else:
                nc.gpsimd.tensor_scalar(dst, src, 1.0, 0.0, ALU.mult, ALU.add)

        def cast_shares(shares, dst, src):
            at = 0
            for engine, width in shares:
                cast(engine, dst[:, at : at + width], src[:, at : at + width])
                at += width

        ident = keep.tile([P, P], F32, name="ident")
        make_identity(nc, ident[:])

        offsets = keep.tile([P, N // 16], U16, name="offsets")
        nc.sync.dma_start(offsets[:], offs)
        warm = keep.tile([P, 1], F32, name="warm")
        nc.vector.memset(warm[:], 0.0)
        nc.scalar.activation(warm[:], warm[:], ACT.Exp)
        kb_win = keep.tile([P, T], F32, name="kb_win")
        nc.sync.dma_start(out=kb_win[:32, :], in_=kb[:32, :])
        nc.vector.memset(kb_win[32:64, :], 0.0)
        nc.vector.memset(kb_win[64:, :], 0.0)
        vs_win = keep.tile([P, T], F32, name="vs_win")
        nc.sync.dma_start(out=vs_win[:32, :], in_=vs[:32, :])
        nc.gpsimd.memset(vs_win[32:64, :], 0.0)
        nc.gpsimd.memset(vs_win[64:, :], 0.0)
        q_raw = keep.tile([P, PASSES, 4, NQ], F32, name="q_raw")
        k_rows = kT.rearrange("(g p t) n -> g p t n", g=PASSES, t=4)
        k_raw = {}
        for (g, u), pieces in SHARES.items():
            for a, b, shares in pieces:
                raw = keep.tile([P, 2, b - a], F32, name=f"k_raw_{g}_{u}_{a}")
                nc.sync.dma_start(out=raw[:], in_=k_rows[g][:, 2 * u : 2 * u + 2, a:b])
                k_raw[(g, u, a)] = raw
        nc.sync.dma_start(out=q_raw[:], in_=qT.rearrange("b (g p t) n -> p (b g) t n", g=PASSES, t=4))
        v_raw = []
        for a, b, shares in V_SHARES:
            raw = keep.tile([P, 2, b - a], F32, name=f"v_raw_{a}", tag=f"v_raw_{b}")
            nc.sync.dma_start(out=raw[:], in_=vT.rearrange("(p h) n -> p h n", h=2)[:, :, a:b])
            v_raw.append(raw)

        ident_bf = keep.tile([P, P], BF16, name="ident_bf")
        make_identity(nc, ident_bf[:])

        def spread(window, name):
            picked = keep.tile([P, N], F32, name=f"{name}_picked")
            nc.vector.tensor_copy(picked[:], window[:].indirect(offsets[:]))
            turned = psum.tile([P, 4, P], F32, name=f"{name}_turned", tag=f"{name}_turned")
            for c in range(4):
                nc.tensor.transpose(turned[:, c, :], picked[:, c * P : (c + 1) * P], ident[:])
            col = keep.tile([P, 4], F32, name=f"{name}_col")
            nc.scalar.activation(col[:], turned[:, :, 0], ACT.Copy)
            rows = psum.tile([P, 4, P], F32, name=f"{name}_rows")
            for c in range(4):
                nc.tensor.transpose(rows[:, c, :], col[:, c : c + 1].to_broadcast([P, P]), ident[:])
            return rows[:].rearrange("p c n -> p (c n)")

        kb_rows = spread(kb_win, "kb")
        vs_g = spread(vs_win, "vs")

        kb_g = keep.tile([P, N], F32, name="kb_g")
        k_g = [keep.tile([P, N * 4], BF16, name=f"k_g{g}", align_bytes=64) for g in range(PASSES)]
        k_words = [keep.tile([P, 2, N], U32, name=f"k_words{g}") for g in range(PASSES)]
        k_codes = [keep.tile([P, N], U32, name=f"k_codes{g}", align_bytes=64) for g in range(PASSES)]
        k_scales = [keep.tile([P, N], U8, name=f"k_scales{g}", align_bytes=64) for g in range(PASSES)]

        def interleave_keys(g, cols):
            dst = k_g[g][:].bitcast(I32).rearrange("p (n u) -> p n u", u=2)[:, cols, :]
            src = k_words[g][:].rearrange("p u n -> p (u n)").bitcast(I32).rearrange("p (u n) -> p n u", u=2)[:, cols, :]
            nc.vector.tensor_copy(dst, src)

        def quantize_keys(g, cols):
            nc.vector.quantize_mx(
                out=k_codes[g][:, cols].bitcast(FP8X4),
                scales=k_scales[g][:, cols],
                in_=k_g[g][:, cols.start * 4 : cols.stop * 4],
            )

        for (g, u), pieces in SHARES.items():
            pool_bf = keep.tile([P, T], U32, name=f"k_bf_{g}_{u}")
            pairs = pool_bf[:].bitcast(BF16).rearrange("p (n j) -> p n j", j=2)
            for a, b, shares in pieces:
                cast_shares(shares, pairs[:, a:b], k_raw[(g, u, a)][:].rearrange("p j n -> p n j"))
            if (g, u) == (1, 0):
                interleave_keys(0, slice(0, N))
            nc.vector.tensor_copy(k_words[g][:, u, :], pool_bf[:].indirect(offsets[:]))
            if (g, u) == (0, 0):
                nc.scalar.activation(kb_g[:], kb_rows, ACT.Copy)
            if (g, u) == (1, 0):
                quantize_keys(0, slice(0, N))

        q_bf = keep.tile([P, PASSES, NQ, 4], BF16, name="q_bf", align_bytes=64)
        for g in range(PASSES):
            cast("SG"[g], q_bf[:, g], q_raw[:, g].rearrange("p t n -> p n t"))
        q_codes = keep.tile([P, PASSES * NQ], U32, name="q_codes", align_bytes=64)
        q_scales = keep.tile([P, PASSES * NQ], U8, name="q_scales", align_bytes=64)
        nc.vector.quantize_mx(out=q_codes[:].bitcast(FP8X4), scales=q_scales[:], in_=q_bf[:].rearrange("p g n t -> p (g n t)"))

        s_bank = [psum.tile([P, 512], F32, name=f"s_bank{h}", tag=f"{x}_turned") for h, x in enumerate(["kb", "vs"])]
        halves = [slice(h * HALF, (h + 1) * HALF) for h in range(2)]
        for cols in halves:
            interleave_keys(1, cols)
        for h, cols in enumerate(halves):
            quantize_keys(1, cols)
            for g in range(PASSES):
                nc.tensor.matmul_mx(
                    out=s_bank[h][:, :HALF],
                    lhsT=q_codes[:, g * NQ : (g + 1) * NQ].bitcast(FP8X4),
                    lhsT_scale=q_scales[:, g * NQ : (g + 1) * NQ],
                    rhs=k_codes[g][:, cols].bitcast(FP8X4),
                    rhs_scale=k_scales[g][:, cols],
                    start=(g == 0),
                    stop=(g == PASSES - 1),
                )

        v_bf = keep.tile([P, T], U32, name="v_bf")
        v_pairs = v_bf[:].bitcast(BF16).rearrange("p (n h) -> p n h", h=2)
        for (a, b, shares), raw in zip(V_SHARES, v_raw):
            cast_shares(shares, v_pairs[:, a:b], raw[:].rearrange("p h n -> p n h"))

        v_g = keep.tile([P, N], U32, name="v_g", align_bytes=64)
        v_slots = v_g[:].rearrange("p (t s) -> p s t", t=4)
        nc.vector.tensor_copy(v_slots[:, : HALF // 4, :], v_bf[:].indirect(offsets[:, :16]))

        s = keep.tile([P, N], F32, name="s")
        for h in range(2):
            cols = slice(h * HALF, (h + 1) * HALF)
            nc.vector.tensor_tensor(s[:, cols], s_bank[h][:, :HALF], kb_g[:, cols], ALU.add)
        neg_m = keep.tile([P, 1], F32, name="neg_m")
        nc.vector.tensor_reduce(neg_m[:], s[:], AX.X, ALU.max, negate=True)
        p = keep.tile([P, N], F32, name="p", tag="v_raw_1024")
        w = keep.tile([P, N], BF16, name="w", align_bytes=64)
        w_slots = w[:].rearrange("p (t s) -> p s t", t=4)
        parts = [keep.tile([P, 1], F32, name=f"l_part{h}") for h in range(2)]
        for h in range(2):
            cols = slice(h * HALF, (h + 1) * HALF)
            nc.scalar.activation(p[:, cols], s[:, cols], ACT.Exp, bias=neg_m[:], accum_out=parts[h][:])
        nc.vector.tensor_copy(v_slots[:, HALF // 4 :, :], v_bf[:].indirect(offsets[:, 16:32]))
        for h in range(2):
            cols = slice(h * HALF, (h + 1) * HALF)
            nc.vector.tensor_tensor(w_slots[:, h * HALF // 4 : (h + 1) * HALF // 4, :], p[:, cols], vs_g[:, cols], ALU.mult)
        w_bank = psum.tile([P, 4, P], BF16, name="w_bank", padded_shape=[P, 8, P])
        for t in range(4):
            nc.tensor.transpose(w_bank[:, t, :], w[:, t * P : (t + 1) * P], ident_bf[:])
        w_t = keep.tile([P, NQ, 4], BF16, name="w_t", align_bytes=64)
        nc.scalar.copy(w_t[:], w_bank[:].rearrange("p t q -> p q t"))
        w_codes = keep.tile([P, NQ], U32, name="w_codes", align_bytes=64)
        w_scales = keep.tile([P, NQ], U8, name="w_scales", align_bytes=64)
        nc.vector.quantize_mx(out=w_codes[:].bitcast(FP8X4), scales=w_scales[:], in_=w_t[:].rearrange("p q t -> p (q t)"))
        total = keep.tile([P, 1], F32, name="total")
        nc.vector.tensor_tensor(total[:], parts[0][:], parts[1][:], ALU.add)
        inv = keep.tile([P, 1], F32, name="inv")
        nc.vector.reciprocal(inv[:], total[:])

        v_bank = psum.tile([P, 4 * P], F32, name="v_bank")
        for t in range(4):
            nc.tensor.transpose(v_bank[:, t * P : (t + 1) * P], v_g[:, t * P : (t + 1) * P].bitcast(F32), ident[:])
        v_t = keep.tile([P, DV, 4], BF16, name="v_t", align_bytes=64)
        nc.vector.tensor_copy(v_t[:], v_bank[:].bitcast(BF16).rearrange("p (t e) -> p e t", t=4))
        v_codes = keep.tile([P, DV], U32, name="v_codes", align_bytes=64)
        v_scales = keep.tile([P, DV], U8, name="v_scales", align_bytes=64)
        nc.vector.quantize_mx(out=v_codes[:].bitcast(FP8X4), scales=v_scales[:], in_=v_t[:].rearrange("p e t -> p (e t)"))

        y_bank = psum.tile([P, DV], F32, name="y_bank", padded_shape=[P, 512])
        nc.tensor.matmul_mx(
            out=y_bank[:],
            lhsT=w_codes[:].bitcast(FP8X4),
            lhsT_scale=w_scales[:],
            rhs=v_codes[:].bitcast(FP8X4),
            rhs_scale=v_scales[:],
            start=True,
            stop=True,
        )
        y = keep.tile([P, DV], F32, name="y")
        nc.vector.tensor_scalar(y[:], y_bank[:], inv[:], None, ALU.mult)
        nc.sync.dma_start(out=out.rearrange("b q e -> (b q) e"), in_=y[:])
